import numpy as np
import ml_dtypes


def mxq(x, axis, fmt="e4m3"):
    dtype, down = {"e4m3": (ml_dtypes.float8_e4m3fn, 7), "e5m2": (ml_dtypes.float8_e5m2, 14)}[fmt]
    v = np.moveaxis(np.asarray(x, np.float32).astype(ml_dtypes.bfloat16).astype(np.float64), axis, -1)
    blocks = v.reshape(v.shape[:-1] + (-1, 32))
    amax = np.abs(blocks).max(-1, keepdims=True)
    byte = np.maximum(np.where(amax > 0, np.frexp(amax)[1] - 1 + 127, 0) - down, 1)
    scale = np.exp2(byte - 127.0)
    codes = (blocks / scale).astype(np.float32).astype(dtype).astype(np.float64)
    return np.moveaxis((codes * scale).reshape(v.shape), -1, axis)


WIDE = False


def mx_kscale(k):
    if not WIDE:
        return np.ones(k)
    levels = np.array([30, -30])
    if k % 512:
        return np.exp2(np.random.permutation(np.resize(levels, k // 32))).repeat(32)
    a = np.empty((k // 512, 16))
    for p in range(k // 512):
        a[p, :8] = np.random.permutation(np.resize(levels, 8))
        for g in range(8):
            far = levels[np.abs(levels - a[p, g]) >= 10]
            a[p, g + 8] = far[np.random.randint(len(far))]
    return np.exp2(a.ravel()).repeat(32)


BF16 = ml_dtypes.bfloat16


def bf(x):
    return np.asarray(x, np.float32).astype(BF16)


def f64(x):
    return np.asarray(x).astype(np.float64)


E2M1 = np.array([0.0, 0.5, 1.0, 1.5, 2.0, 3.0, 4.0, 6.0, -0.0, -0.5, -1.0, -1.5, -2.0, -3.0, -4.0, -6.0])


def pack_weight(w, fmt):
    k, n = w.shape
    w = f64(bf(w)).reshape(k // 32, 32, n)
    amax = np.abs(w).max(1)
    if fmt == "e4m3":
        byte = np.frexp(amax)[1] - 1 + 127 - 7
    else:
        mant, ex = np.frexp(amax / 6.0)
        byte = np.where(mant > 0.5, ex, ex - 1) + 127
    byte = np.clip(np.where(amax > 0, byte, 1), 1, 254)
    scaled = (w * np.exp2(127.0 - byte)[:, None, :]).reshape(k, n).astype(np.float32)
    by_word = np.ascontiguousarray(scaled.reshape(k // 512, 128, 4, n).transpose(0, 1, 3, 2))
    if fmt == "e4m3":
        words = by_word.astype(ml_dtypes.float8_e4m3fn).view(np.uint8)
    else:
        c = by_word.astype(ml_dtypes.float4_e2m1fn).view(np.uint8) & 0xF
        words = c[..., 0::2] | (c[..., 1::2] << 4)
    return np.ascontiguousarray(words), np.ascontiguousarray(byte.astype(np.uint8).reshape(k // 512, 16, n))


def unpack_weight(words, scales, fmt):
    g, p, n, _ = words.shape
    if fmt == "e4m3":
        vals = np.ascontiguousarray(words).view(ml_dtypes.float8_e4m3fn).astype(np.float64)
    else:
        nib = np.empty((g, p, n, 4), np.uint8)
        nib[..., 0::2] = words & 0xF
        nib[..., 1::2] = words >> 4
        vals = E2M1[nib]
    vals = vals * np.repeat(np.exp2(scales.astype(np.float64) - 127.0), 8, axis=1)[..., None]
    return vals.transpose(0, 1, 3, 2).reshape(g * 512, n)
def pack4(w):
    words, scales = pack_weight(w, "e2m1")
    return words.reshape(words.shape[0], 128, -1), scales


def unpack4(words, scales):
    return unpack_weight(words.reshape(words.shape[0], 128, -1, 2), scales, "e2m1")


M, K, E, D = 1024, 2048, 1024, 2048


def setup_inputs():
    s = mx_kscale(K)
    t = mx_kscale(E)
    x = np.random.standard_normal((M, K)) * s
    own = np.random.standard_normal((K, E))
    common = np.random.standard_normal((K, 1))
    w = (own + 0.5 * common) / np.sqrt(K) / s[:, None]
    w_words, w_scales = pack4(w)
    gain = (1 + 0.1 * np.random.standard_normal(E)) * t
    v = np.random.standard_normal((E, D)) / np.sqrt(E) / t[:, None]
    return {"x": bf(x), "w_words": w_words, "w_scales": w_scales,
            "gain": bf(gain), "v": bf(v)}


def reference(x, w_words, w_scales, gain, v):
    z = mxq(f64(x), 1, "e4m3") @ unpack4(w_words, w_scales)
    a = 1 / (1 + np.exp(-z))
    h = a * f64(gain)
    y = mxq(h, 1, "e5m2") @ mxq(f64(v), 0, "e4m3")
    return y / np.mean(a, axis=1, keepdims=True)

@@ -1,0 +1,311 @@
+from contextlib import ExitStack
+
+import concourse.mybir as mybir
+from concourse.masks import make_identity
+
+M, K, E, D = 1024, 2048, 1024, 2048
+FLOPS = 2 * M * K * E + 2 * M * E * D
+
+F32 = mybir.dt.float32
+BF16 = mybir.dt.bfloat16
+I32 = mybir.dt.int32
+U32 = mybir.dt.uint32
+U8 = mybir.dt.uint8
+E4M3X4 = mybir.dt.float8_e4m3fn_x4
+E5M2X4 = mybir.dt.float8_e5m2_x4
+E2M1X4 = mybir.dt.float4_e2m1fn_x4
+ACT = mybir.ActivationFunctionType
+ALU = mybir.AluOpType
+
+P = 128
+PACK = 4
+K_PASS = P * PACK
+K_PASSES = K // K_PASS
+E_PASSES = E // K_PASS
+TILES = M // P
+BANK = 512
+QUARTERS = D // BANK
+
+
+def tile_sigmoid_router_bias_mix_s9_kernel(tc, x, w_words, w_scales, gain, v, out):
+    nc = tc.nc
+    with ExitStack() as ctx:
+        keep = ctx.enter_context(tc.tile_pool(name="keep", bufs=1))
+        work = ctx.enter_context(tc.tile_pool(name="work", bufs=3))
+        psum = ctx.enter_context(tc.psum_pool(name="psum", bufs=8))
+
+        x_raw = [keep.tile([P, K], BF16, name="x_raw_%d" % i, align_bytes=64) for i in range(TILES)]
+        v_raw = [
+            [keep.tile([P, PACK, D // 2], BF16, name="v_raw_%d_%d" % (g, h), align_bytes=64) for h in range(2)]
+            for g in range(E_PASSES)
+        ]
+        w_codes = keep.tile([P, K_PASSES, 2 * E], U8, name="w_codes", align_bytes=64)
+        w_planes = keep.tile([P, K_PASSES, E], U8, name="w_planes", align_bytes=64)
+        v_codes = [
+            [keep.tile([P, BANK], U32, name="v_codes_%d_%d" % (g, q), align_bytes=64) for q in range(QUARTERS)]
+            for g in range(E_PASSES)
+        ]
+        v_planes = [
+            [keep.tile([P, BANK], U8, name="v_planes_%d_%d" % (g, q), align_bytes=64) for q in range(QUARTERS)]
+            for g in range(E_PASSES)
+        ]
+        h_codes = [keep.tile([P, E_PASSES * P], U32, name="h_codes_%d" % i, align_bytes=64) for i in range(TILES)]
+        h_planes = [keep.tile([P, E_PASSES * P], U8, name="h_planes_%d" % i, align_bytes=64) for i in range(TILES)]
+        inv_mean = [keep.tile([P, 1], F32, name="inv_mean_%d" % i) for i in range(TILES)]
+        gain_row = keep.tile([P, E], BF16, name="gain_row")
+        gain_all = keep.tile([P, E], F32, name="gain_all")
+        ones = keep.tile([P, P], BF16, name="ones")
+        ident = keep.tile([P, P], F32, name="ident")
+        warm = keep.tile([P, 1], F32, name="warm")
+
+        with tc.manual_schedule():
+            nc.vector.memset(warm[:], 0.0)
+            nc.vector.memset(w_planes[:].rearrange("p g n -> p (g n)").bitcast(I32), 0)
+            make_identity(nc, ident[:])
+            nc.gpsimd.memset(gain_row[:], 0.0)
+            nc.gpsimd.dma_start(out=gain_row[0:1, :], in_=gain.rearrange("(o e) -> o e", o=1))
+            nc.gpsimd.memset(ones[:], 1.0)
+            nc.scalar.activation(out=warm[:], in_=warm[:], func=ACT.Sigmoid)
+
+            def load_x(i, parts=1):
+                width = K // parts
+                for c in range(parts):
+                    cols = slice(c * width, (c + 1) * width)
+                    nc.sync.dma_start(out=x_raw[i][:, cols], in_=x[i * P : (i + 1) * P, cols])
+
+            def load_v(g, h):
+                rows = v[g * K_PASS : (g + 1) * K_PASS, h * (D // 2) : (h + 1) * (D // 2)]
+                nc.sync.dma_start(out=v_raw[g][h][:], in_=rows.rearrange("(p j) d -> p j d", j=PACK))
+
+            def load_w(g):
+                nc.sync.dma_start(
+                    out=w_codes[:, g : g + 2, :].bitcast(I32),
+                    in_=w_words[g : g + 2].rearrange("g p b -> p g b").bitcast(I32),
+                )
+
+            load_x(0)
+            for quad in range(4):
+                nc.sync.dma_start(
+                    out=w_planes[32 * quad : 32 * quad + 4, :, :].bitcast(I32),
+                    in_=w_scales[:, 4 * quad : 4 * quad + 4, :].rearrange("g r n -> r g n").bitcast(I32),
+                )
+            load_x(1)
+            load_w(0)
+            load_w(2)
+            load_x(2)
+            load_v(0, 0)
+            load_x(3)
+            load_v(1, 0)
+            for i in range(4, TILES):
+                load_x(i)
+            load_v(0, 1)
+            load_v(1, 1)
+
+            x_codes = {}
+            x_planes = {}
+            x_grouped = {}
+            a_tiles = {}
+            h_tiles = {}
+            row_sums = {}
+            v_grouped = {}
+            means = {}
+            y_tiles = {}
+
+            def transpose_x(i):
+                words = x_raw[i][:].bitcast(F32)
+                x_grouped[i] = work.tile([P, K_PASSES, P, PACK], BF16, name="x_grouped", align_bytes=64)
+                for b in range(2):
+                    bank = psum.tile([P, 2, 2, P], F32, name="bank")
+                    for gg in range(2):
+                        for u in range(2):
+                            first = 256 * (2 * b + gg) + u
+                            nc.tensor.transpose(bank[:, gg, u, :], words[:, first : first + 255 : 2], ident[:])
+                    dst = x_grouped[i][:, 2 * b : 2 * b + 2].rearrange("p g r t -> p g (r t)").bitcast(F32)
+                    dst = dst.rearrange("p g (r u) -> p g r u", u=2)
+                    src = bank[:].rearrange("p g u r -> p g r u")
+                    if b == 0 and i < 2:
+                        nc.vector.tensor_copy(out=dst, in_=src)
+                    else:
+                        nc.scalar.copy(out=dst, in_=src)
+
+            def quantise_x(i):
+                x_codes[i] = work.tile([P, K_PASSES * P], U32, name="x_codes", align_bytes=64)
+                x_planes[i] = work.tile([P, K_PASSES * P], U8, name="x_planes", align_bytes=64)
+                nc.vector.quantize_mx(
+                    out=x_codes[i][:].bitcast(E4M3X4),
+                    scales=x_planes[i][:],
+                    in_=x_grouped[i][:].rearrange("p g r t -> p (g r t)"),
+                )
+
+            banks = {}
+
+            def logits_passes(i, half, passes):
+                if passes[0] == 0:
+                    banks[half] = psum.tile([P, BANK], F32, name="bank")
+                for g in passes:
+                    bank = banks[half]
+                    rows = slice(g * P, (g + 1) * P)
+                    nc.tensor.matmul_mx(
+                        out=bank[:],
+                        lhsT=x_codes[i][:, rows].bitcast(E4M3X4),
+                        lhsT_scale=x_planes[i][:, rows],
+                        rhs=w_codes[:, g, 2 * half * BANK : 2 * (half + 1) * BANK].bitcast(E2M1X4),
+                        rhs_scale=w_planes[:, g, half * BANK : (half + 1) * BANK],
+                        start=(g == 0),
+                        stop=(g == K_PASSES - 1),
+                    )
+
+            def affinities(i, half):
+                bank = banks[half]
+                if half == 0:
+                    a_tiles[i] = work.tile([P, E], F32, name="a")
+                    row_sums[i] = work.tile([P, 2], F32, name="row_sums")
+                nc.scalar.activation(
+                    out=a_tiles[i][:, half * BANK : (half + 1) * BANK],
+                    in_=bank[:],
+                    func=ACT.Sigmoid,
+                    accum_out=row_sums[i][:, half : half + 1],
+                )
+
+            def apply_gain(i, half):
+                if half == 0:
+                    h_tiles[i] = work.tile([P, E], BF16, name="h", align_bytes=64)
+                cols = slice(half * BANK, (half + 1) * BANK)
+                nc.vector.tensor_tensor(
+                    out=h_tiles[i][:, cols].rearrange("q (u p e) -> q u p e", u=2, e=2),
+                    in0=a_tiles[i][:, cols].rearrange("q (p u e) -> q u p e", u=2, e=2),
+                    in1=gain_all[:, cols].rearrange("q (u p e) -> q u p e", u=2, e=2),
+                    op=ALU.mult,
+                )
+
+            def finish_mean(i):
+                means[i] = work.tile([P, 1], F32, name="mean")
+                nc.vector.tensor_scalar(
+                    out=means[i][:], in0=row_sums[i][:, 0:1], scalar1=row_sums[i][:, 1:2], scalar2=1.0 / E, op0=ALU.add, op1=ALU.mult
+                )
+
+            def invert_mean(i):
+                nc.vector.reciprocal(out=inv_mean[i][:], in_=means[i][:])
+
+            h_grouped = {}
+
+            def transpose_h(i):
+                words = h_tiles[i][:].bitcast(F32)
+                bank = psum.tile([P, 2, 2, P], F32, name="bank")
+                for g in range(2):
+                    for u in range(2):
+                        first = P * (2 * g + u)
+                        nc.tensor.transpose(bank[:, g, u, :], words[:, first : first + P], ident[:])
+                h_grouped[i] = work.tile([P, E_PASSES, P, PACK], BF16, name="h_grouped", align_bytes=64)
+                dst = h_grouped[i][:].rearrange("p g r t -> p g (r t)").bitcast(F32)
+                nc.scalar.copy(out=dst.rearrange("p g (r u) -> p g r u", u=2), in_=bank[:].rearrange("p g u r -> p g r u"))
+
+            def quantise_h(i):
+                nc.vector.quantize_mx(
+                    out=h_codes[i][:].bitcast(E5M2X4),
+                    scales=h_planes[i][:],
+                    in_=h_grouped[i][:].rearrange("p g r t -> p (g r t)"),
+                )
+
+            def group_v(g, q):
+                v_grouped[g, q] = work.tile([P, BANK, PACK], BF16, name="v_grouped", align_bytes=64)
+                first = (q % 2) * BANK
+                nc.vector.tensor_copy(
+                    out=v_grouped[g, q][:],
+                    in_=v_raw[g][q // 2][:, :, first : first + BANK].rearrange("p j d -> p d j"),
+                )
+
+            def quantise_v(g, q):
+                nc.vector.quantize_mx(
+                    out=v_codes[g][q][:].bitcast(E4M3X4),
+                    scales=v_planes[g][q][:],
+                    in_=v_grouped[g, q][:].rearrange("p d j -> p (d j)"),
+                )
+
+            def mix(i, half, share, last=False):
+                y = work.tile([P, 2 * BANK], F32, name="y", bufs=8)
+                for qq in range(2):
+                    q = 2 * half + qq
+                    bank = psum.tile([P, BANK], F32, name="bank")
+                    for g in range(E_PASSES):
+                        rows = slice(g * P, (g + 1) * P)
+                        nc.tensor.matmul_mx(
+                            out=bank[:],
+                            lhsT=h_codes[i][:, rows].bitcast(E5M2X4),
+                            lhsT_scale=h_planes[i][:, rows],
+                            rhs=v_codes[g][q][:].bitcast(E4M3X4),
+                            rhs_scale=v_planes[g][q][:],
+                            start=(g == 0),
+                            stop=(g == E_PASSES - 1),
+                        )
+                    dst = y[:, qq * BANK : (qq + 1) * BANK]
+                    if qq == 0 or not share:
+                        nc.scalar.activation(out=dst, in_=bank[:], func=ACT.Copy, scale=inv_mean[i][:])
+                    else:
+                        nc.vector.tensor_scalar(out=dst, in0=bank[:], scalar1=inv_mean[i][:], scalar2=None, op0=ALU.mult)
+                    if last:
+                        nc.sync.dma_start(out=out[i * P : (i + 1) * P, q * BANK : (q + 1) * BANK], in_=dst)
+                if not last:
+                    nc.sync.dma_start(
+                        out=out[i * P : (i + 1) * P, half * 2 * BANK : (half + 1) * 2 * BANK], in_=y[:]
+                    )
+
+            transpose_x(0)
+            quantise_x(0)
+            for g in range(2):
+                bank = psum.tile([P, BANK], F32, name="bank")
+                nc.tensor.matmul(bank[:], lhsT=ones[:], rhs=gain_row[:, g * BANK : (g + 1) * BANK], start=True, stop=True)
+                nc.vector.tensor_copy(
+                    out=gain_all[:, g * BANK : (g + 1) * BANK].rearrange("q (u p e) -> q u p e", u=2, e=2),
+                    in_=bank[:].rearrange("q (p u e) -> q u p e", u=2, e=2),
+                )
+            transpose_x(1)
+
+            v_plan = {1: [(0, 0)], 2: [(0, 1), (1, 0)], 3: [(1, 1)], 4: [(0, 2)], 5: [(1, 2)], 6: [(0, 3)], 7: [(1, 3)]}
+            y_plan = {
+                4: [(0, 0)], 5: [(1, 0), (2, 0)], 6: [(3, 0), (4, 0)], 7: [(5, 0)],
+            }
+            for s in range(TILES + 1):
+                units = v_plan.get(s, [])
+                if s == 0:
+                    for half in range(2):
+                        logits_passes(0, half, (0, 1))
+                    logits_passes(0, 0, (2, 3))
+                    affinities(0, 0)
+                elif s < TILES:
+                    logits_passes(s, 0, range(K_PASSES))
+                    affinities(s, 0)
+                if 1 <= s + 1 < TILES:
+                    quantise_x(s + 1)
+                if s >= 2:
+                    quantise_h(s - 2)
+                if units:
+                    group_v(*units[0])
+                if s < TILES:
+                    logits_passes(s, 1, (2, 3) if s == 0 else range(K_PASSES))
+                    affinities(s, 1)
+                    apply_gain(s, 0)
+                if units:
+                    quantise_v(*units[0])
+                if s + 2 < TILES:
+                    transpose_x(s + 2)
+                if len(units) > 1:
+                    group_v(*units[1])
+                if s < TILES:
+                    apply_gain(s, 1)
+                    finish_mean(s)
+                if s >= 1:
+                    transpose_h(s - 1)
+                if len(units) > 1:
+                    quantise_v(*units[1])
+                if s < TILES:
+                    invert_mean(s)
+                for i, half in y_plan.get(s, []):
+                    mix(i, half, False)
+            mix(6, 0, True)
+            mix(0, 1, True)
+            quantise_h(7)
+            mix(1, 1, True)
+            mix(7, 0, True)
+            for i in range(2, TILES):
+                mix(i, 1, True, i == TILES - 1)

@@ -14,17 +14,26 @@ U8 = mybir.dt.uint8
 E4M3X4 = mybir.dt.float8_e4m3fn_x4
 E5M2X4 = mybir.dt.float8_e5m2_x4
 E2M1X4 = mybir.dt.float4_e2m1fn_x4
-ACT = mybir.ActivationFunctionType
-ALU = mybir.AluOpType
+SIGMOID = mybir.ActivationFunctionType.Sigmoid
+COPY = mybir.ActivationFunctionType.Copy
+ADD = mybir.AluOpType.add
+MULT = mybir.AluOpType.mult
 
 P = 128
 PACK = 4
 K_PASS = P * PACK
-K_PASSES = K // K_PASS
-E_PASSES = E // K_PASS
+X_PASSES = K // K_PASS
+H_PASSES = E // K_PASS
 TILES = M // P
 BANK = 512
 QUARTERS = D // BANK
+HALF = 2 * BANK
+
+V_STEP = {(0, 0): 1, (1, 0): 2, (0, 1): 3, (1, 1): 3, (0, 2): 4, (1, 2): 5, (0, 3): 6, (1, 3): 7}
+V_ON_SCALAR = (0, 2)
+MIXES_IN_STEP = {4: 1, 5: 2, 6: 2, 7: 2}
+MEANS_AFTER_STEP = {3: (0, 4), 5: (4, 6), 7: (6, 8)}
+DUMMIES = (4, 1, 2)
 
 
 def tile_sigmoid_router_bias_mix_s9_kernel(tc, x, w_words, w_scales, gain, v, out):
@@ -36,276 +45,297 @@ def tile_sigmoid_router_bias_mix_s9_kernel(tc, x, w_words, w_scales, gain, v, ou
 
         x_raw = [keep.tile([P, K], BF16, name="x_raw_%d" % i, align_bytes=64) for i in range(TILES)]
         v_raw = [
-            [keep.tile([P, PACK, D // 2], BF16, name="v_raw_%d_%d" % (g, h), align_bytes=64) for h in range(2)]
-            for g in range(E_PASSES)
+            [keep.tile([P, PACK, HALF], BF16, name="v_raw_%d_%d" % (g, h), align_bytes=64) for h in range(D // HALF)]
+            for g in range(H_PASSES)
         ]
-        w_codes = keep.tile([P, K_PASSES, 2 * E], U8, name="w_codes", align_bytes=64)
-        w_planes = keep.tile([P, K_PASSES, E], U8, name="w_planes", align_bytes=64)
+        w_codes = keep.tile([P, X_PASSES, 2 * E], U8, name="w_codes", align_bytes=64)
+        w_planes = keep.tile([P, X_PASSES, E], U8, name="w_planes", align_bytes=64)
         v_codes = [
             [keep.tile([P, BANK], U32, name="v_codes_%d_%d" % (g, q), align_bytes=64) for q in range(QUARTERS)]
-            for g in range(E_PASSES)
+            for g in range(H_PASSES)
         ]
         v_planes = [
             [keep.tile([P, BANK], U8, name="v_planes_%d_%d" % (g, q), align_bytes=64) for q in range(QUARTERS)]
-            for g in range(E_PASSES)
+            for g in range(H_PASSES)
         ]
-        h_codes = [keep.tile([P, E_PASSES * P], U32, name="h_codes_%d" % i, align_bytes=64) for i in range(TILES)]
-        h_planes = [keep.tile([P, E_PASSES * P], U8, name="h_planes_%d" % i, align_bytes=64) for i in range(TILES)]
-        inv_mean = [keep.tile([P, 1], F32, name="inv_mean_%d" % i) for i in range(TILES)]
+        h_codes = [keep.tile([P, H_PASSES * P], U32, name="h_codes_%d" % i, align_bytes=64) for i in range(TILES)]
+        h_planes = [keep.tile([P, H_PASSES * P], U8, name="h_planes_%d" % i, align_bytes=64) for i in range(TILES)]
+        row_sums = keep.tile([P, H_PASSES, TILES], F32, name="row_sums")
+        row_sum = keep.tile([P, TILES], F32, name="row_sum")
+        mean = keep.tile([P, TILES], F32, name="mean")
+        inv_mean = keep.tile([P, TILES], F32, name="inv_mean")
         gain_row = keep.tile([P, E], BF16, name="gain_row")
         gain_all = keep.tile([P, E], F32, name="gain_all")
+        dummy_rhs = keep.tile([P, BANK], BF16, name="dummy_rhs")
         ones = keep.tile([P, P], BF16, name="ones")
         ident = keep.tile([P, P], F32, name="ident")
-        warm = keep.tile([P, 1], F32, name="warm")
+        table_loader = keep.tile([P, 1], F32, name="table_loader")
+
+        x_grouped, x_codes, x_planes = {}, {}, {}
+        logit_banks, affinity, h_tiles, h_grouped, v_grouped = {}, {}, {}, {}, {}
+
+
+        def load_x(i, parts=1):
+            width = K // parts
+            for c in range(parts):
+                cols = slice(c * width, (c + 1) * width)
+                nc.sync.dma_start(out=x_raw[i][:, cols], in_=x[i * P : (i + 1) * P, cols])
+
+        def load_w_scales():
+            for quadrant in range(4):
+                nc.sync.dma_start(
+                    out=w_planes[32 * quadrant : 32 * quadrant + 4, :, :].bitcast(I32),
+                    in_=w_scales[:, 4 * quadrant : 4 * quadrant + 4, :].rearrange("g r n -> r g n").bitcast(I32),
+                )
+
+        def load_w_pair(g):
+            nc.sync.dma_start(
+                out=w_codes[:, g : g + 2, :].bitcast(I32),
+                in_=w_words[g : g + 2].rearrange("g p b -> p g b").bitcast(I32),
+            )
+
+        def load_v(g, h):
+            piece = v[g * K_PASS : (g + 1) * K_PASS, h * HALF : (h + 1) * HALF]
+            nc.sync.dma_start(out=v_raw[g][h][:], in_=piece.rearrange("(p j) d -> p j d", j=PACK))
+
+
+        def dummy_matmuls(count):
+            bank = psum.tile([P, BANK], F32, name="bank")
+            for n in range(count):
+                nc.tensor.matmul(bank[:], lhsT=ones[:], rhs=dummy_rhs[:], start=True, stop=True)
+
+        def spread_gain():
+            for g in range(H_PASSES):
+                cols = slice(g * K_PASS, (g + 1) * K_PASS)
+                bank = psum.tile([P, BANK], F32, name="bank")
+                nc.tensor.matmul(bank[:], lhsT=ones[:], rhs=gain_row[:, cols], start=True, stop=True)
+                nc.vector.tensor_copy(
+                    out=gain_all[:, cols].rearrange("q (u p e) -> q u p e", u=2, e=2),
+                    in_=bank[:].rearrange("q (p u e) -> q u p e", u=2, e=2),
+                )
+
+
+        def transpose_x(i):
+            words = x_raw[i][:].bitcast(F32)
+            x_grouped[i] = work.tile([P, X_PASSES, P, PACK], BF16, name="x_grouped", align_bytes=64)
+            for pair in range(X_PASSES // 2):
+                bank = psum.tile([P, 2, 2, P], F32, name="bank")
+                for g in range(2):
+                    for u in range(2):
+                        first = (2 * pair + g) * K_PASS // 2 + u
+                        nc.tensor.transpose(bank[:, g, u, :], words[:, first : first + K_PASS // 2 - 1 : 2], ident[:])
+                grouped = x_grouped[i][:, 2 * pair : 2 * pair + 2].rearrange("p g r t -> p g (r t)").bitcast(F32)
+                dst = grouped.rearrange("p g (r u) -> p g r u", u=2)
+                src = bank[:].rearrange("p g u r -> p g r u")
+                if i == 0 and pair == 0:
+                    nc.vector.tensor_copy(out=dst, in_=src)
+                else:
+                    nc.scalar.copy(out=dst, in_=src)
+
+        def quantise_x(i):
+            x_codes[i] = work.tile([P, X_PASSES * P], U32, name="x_codes", align_bytes=64)
+            x_planes[i] = work.tile([P, X_PASSES * P], U8, name="x_planes", align_bytes=64)
+            nc.vector.quantize_mx(
+                out=x_codes[i][:].bitcast(E4M3X4),
+                scales=x_planes[i][:],
+                in_=x_grouped[i][:].rearrange("p g r t -> p (g r t)"),
+            )
+
+        def logits(i, half, passes):
+            if passes[0] == 0:
+                logit_banks[half] = psum.tile([P, BANK], F32, name="bank")
+            for g in passes:
+                tokens = slice(g * P, (g + 1) * P)
+                nc.tensor.matmul_mx(
+                    out=logit_banks[half][:],
+                    lhsT=x_codes[i][:, tokens].bitcast(E4M3X4),
+                    lhsT_scale=x_planes[i][:, tokens],
+                    rhs=w_codes[:, g, 2 * half * BANK : 2 * (half + 1) * BANK].bitcast(E2M1X4),
+                    rhs_scale=w_planes[:, g, half * BANK : (half + 1) * BANK],
+                    start=(g == 0),
+                    stop=(g == X_PASSES - 1),
+                )
+
+        def sigmoid(i, half):
+            if half == 0:
+                affinity[i] = work.tile([P, E], F32, name="affinity")
+            nc.scalar.activation(
+                out=affinity[i][:, half * BANK : (half + 1) * BANK],
+                in_=logit_banks[half][:],
+                func=SIGMOID,
+                accum_out=row_sums[:, half, i : i + 1],
+            )
+
+        def apply_gain(i, half):
+            if half == 0:
+                h_tiles[i] = work.tile([P, E], BF16, name="h", align_bytes=64)
+            cols = slice(half * BANK, (half + 1) * BANK)
+            nc.vector.tensor_tensor(
+                out=h_tiles[i][:, cols].rearrange("q (u p e) -> q u p e", u=2, e=2),
+                in0=affinity[i][:, cols].rearrange("q (p u e) -> q u p e", u=2, e=2),
+                in1=gain_all[:, cols].rearrange("q (u p e) -> q u p e", u=2, e=2),
+                op=MULT,
+            )
+
+        def add_row_sums(tiles):
+            nc.vector.tensor_tensor(
+                out=row_sum[:, tiles], in0=row_sums[:, 0, tiles], in1=row_sums[:, 1, tiles], op=ADD
+            )
+
+        def divide_by_experts(tiles):
+            nc.vector.tensor_scalar(
+                out=mean[:, tiles], in0=row_sum[:, tiles], scalar1=1.0 / E, scalar2=None, op0=MULT
+            )
+
+        def invert_mean(tiles):
+            nc.vector.reciprocal(out=inv_mean[:, tiles], in_=mean[:, tiles])
+
+
+        def transpose_h(i):
+            words = h_tiles[i][:].bitcast(F32)
+            bank = psum.tile([P, H_PASSES, 2, P], F32, name="bank")
+            for g in range(H_PASSES):
+                for u in range(2):
+                    first = P * (2 * g + u)
+                    nc.tensor.transpose(bank[:, g, u, :], words[:, first : first + P], ident[:])
+            h_grouped[i] = work.tile([P, H_PASSES, P, PACK], BF16, name="h_grouped", align_bytes=64)
+            grouped = h_grouped[i][:].rearrange("p g r t -> p g (r t)").bitcast(F32)
+            nc.scalar.copy(out=grouped.rearrange("p g (r u) -> p g r u", u=2), in_=bank[:].rearrange("p g u r -> p g r u"))
+
+        def quantise_h(i):
+            nc.vector.quantize_mx(
+                out=h_codes[i][:].bitcast(E5M2X4),
+                scales=h_planes[i][:],
+                in_=h_grouped[i][:].rearrange("p g r t -> p (g r t)"),
+            )
+
+        def interleave_v(g, q):
+            v_grouped[g, q] = work.tile([P, BANK, PACK], BF16, name="v_grouped", align_bytes=64)
+            first = (q % 2) * BANK
+            copy = nc.scalar.copy if (g, q) == V_ON_SCALAR else nc.vector.tensor_copy
+            copy(
+                out=v_grouped[g, q][:].rearrange("p (c i) j -> p c j i", i=4),
+                in_=v_raw[g][q // 2][:, :, first : first + BANK].rearrange("p j (c i) -> p c j i", i=4),
+            )
+
+        def quantise_v(g, q):
+            nc.vector.quantize_mx(
+                out=v_codes[g][q][:].bitcast(E4M3X4),
+                scales=v_planes[g][q][:],
+                in_=v_grouped[g, q][:].rearrange("p d j -> p (d j)"),
+            )
+
+
+        def mix(i, half, engines, store_quarters=False):
+            rows = slice(i * P, (i + 1) * P)
+            y = work.tile([P, HALF], F32, name="y", bufs=8)
+            for b in range(2):
+                q = 2 * half + b
+                bank = psum.tile([P, BANK], F32, name="bank")
+                for g in range(H_PASSES):
+                    tokens = slice(g * P, (g + 1) * P)
+                    nc.tensor.matmul_mx(
+                        out=bank[:],
+                        lhsT=h_codes[i][:, tokens].bitcast(E5M2X4),
+                        lhsT_scale=h_planes[i][:, tokens],
+                        rhs=v_codes[g][q][:].bitcast(E4M3X4),
+                        rhs_scale=v_planes[g][q][:],
+                        start=(g == 0),
+                        stop=(g == H_PASSES - 1),
+                    )
+                dst = y[:, b * BANK : (b + 1) * BANK]
+                inverse = inv_mean[:, i : i + 1]
+                if engines[b] == "scalar":
+                    nc.scalar.activation(out=dst, in_=bank[:], func=COPY, scale=inverse)
+                else:
+                    nc.vector.tensor_scalar(out=dst, in0=bank[:], scalar1=inverse, scalar2=None, op0=MULT)
+                if store_quarters:
+                    nc.sync.dma_start(out=out[rows, q * BANK : (q + 1) * BANK], in_=dst)
+            if not store_quarters:
+                nc.sync.dma_start(out=out[rows, half * HALF : (half + 1) * HALF], in_=y[:])
+
 
         with tc.manual_schedule():
-            nc.vector.memset(warm[:], 0.0)
-            nc.vector.memset(w_planes[:].rearrange("p g n -> p (g n)").bitcast(I32), 0)
+            nc.vector.memset(table_loader[:], 0.0)
             make_identity(nc, ident[:])
-            nc.gpsimd.memset(gain_row[:], 0.0)
-            nc.gpsimd.dma_start(out=gain_row[0:1, :], in_=gain.rearrange("(o e) -> o e", o=1))
-            nc.gpsimd.memset(ones[:], 1.0)
-            nc.scalar.activation(out=warm[:], in_=warm[:], func=ACT.Sigmoid)
+            nc.vector.memset(ones[:], 1.0)
+            nc.vector.memset(dummy_rhs[:], 0.0)
+            nc.vector.memset(w_planes[:].rearrange("p g n -> p (g n)").bitcast(I32), 0)
+            nc.vector.memset(gain_row[:], 0.0)
+            nc.scalar.activation(out=table_loader[:], in_=table_loader[:], func=SIGMOID)
 
-            def load_x(i, parts=1):
-                width = K // parts
-                for c in range(parts):
-                    cols = slice(c * width, (c + 1) * width)
-                    nc.sync.dma_start(out=x_raw[i][:, cols], in_=x[i * P : (i + 1) * P, cols])
-
-            def load_v(g, h):
-                rows = v[g * K_PASS : (g + 1) * K_PASS, h * (D // 2) : (h + 1) * (D // 2)]
-                nc.sync.dma_start(out=v_raw[g][h][:], in_=rows.rearrange("(p j) d -> p j d", j=PACK))
-
-            def load_w(g):
-                nc.sync.dma_start(
-                    out=w_codes[:, g : g + 2, :].bitcast(I32),
-                    in_=w_words[g : g + 2].rearrange("g p b -> p g b").bitcast(I32),
-                )
-
-            load_x(0)
-            for quad in range(4):
-                nc.sync.dma_start(
-                    out=w_planes[32 * quad : 32 * quad + 4, :, :].bitcast(I32),
-                    in_=w_scales[:, 4 * quad : 4 * quad + 4, :].rearrange("g r n -> r g n").bitcast(I32),
-                )
+            load_x(0, parts=2)
             load_x(1)
-            load_w(0)
-            load_w(2)
+            load_w_scales()
+            load_w_pair(0)
+            load_w_pair(2)
+            nc.sync.dma_start(out=gain_row[0:1, :], in_=gain.rearrange("(o e) -> o e", o=1))
             load_x(2)
-            load_v(0, 0)
             load_x(3)
+            load_v(0, 0)
+            load_x(4)
             load_v(1, 0)
-            for i in range(4, TILES):
+            for i in range(5, TILES):
                 load_x(i)
             load_v(0, 1)
             load_v(1, 1)
 
-            x_codes = {}
-            x_planes = {}
-            x_grouped = {}
-            a_tiles = {}
-            h_tiles = {}
-            row_sums = {}
-            v_grouped = {}
-            means = {}
-            y_tiles = {}
-
-            def transpose_x(i):
-                words = x_raw[i][:].bitcast(F32)
-                x_grouped[i] = work.tile([P, K_PASSES, P, PACK], BF16, name="x_grouped", align_bytes=64)
-                for b in range(2):
-                    bank = psum.tile([P, 2, 2, P], F32, name="bank")
-                    for gg in range(2):
-                        for u in range(2):
-                            first = 256 * (2 * b + gg) + u
-                            nc.tensor.transpose(bank[:, gg, u, :], words[:, first : first + 255 : 2], ident[:])
-                    dst = x_grouped[i][:, 2 * b : 2 * b + 2].rearrange("p g r t -> p g (r t)").bitcast(F32)
-                    dst = dst.rearrange("p g (r u) -> p g r u", u=2)
-                    src = bank[:].rearrange("p g u r -> p g r u")
-                    if b == 0 and i < 2:
-                        nc.vector.tensor_copy(out=dst, in_=src)
-                    else:
-                        nc.scalar.copy(out=dst, in_=src)
-
-            def quantise_x(i):
-                x_codes[i] = work.tile([P, K_PASSES * P], U32, name="x_codes", align_bytes=64)
-                x_planes[i] = work.tile([P, K_PASSES * P], U8, name="x_planes", align_bytes=64)
-                nc.vector.quantize_mx(
-                    out=x_codes[i][:].bitcast(E4M3X4),
-                    scales=x_planes[i][:],
-                    in_=x_grouped[i][:].rearrange("p g r t -> p (g r t)"),
-                )
-
-            banks = {}
-
-            def logits_passes(i, half, passes):
-                if passes[0] == 0:
-                    banks[half] = psum.tile([P, BANK], F32, name="bank")
-                for g in passes:
-                    bank = banks[half]
-                    rows = slice(g * P, (g + 1) * P)
-                    nc.tensor.matmul_mx(
-                        out=bank[:],
-                        lhsT=x_codes[i][:, rows].bitcast(E4M3X4),
-                        lhsT_scale=x_planes[i][:, rows],
-                        rhs=w_codes[:, g, 2 * half * BANK : 2 * (half + 1) * BANK].bitcast(E2M1X4),
-                        rhs_scale=w_planes[:, g, half * BANK : (half + 1) * BANK],
-                        start=(g == 0),
-                        stop=(g == K_PASSES - 1),
-                    )
-
-            def affinities(i, half):
-                bank = banks[half]
-                if half == 0:
-                    a_tiles[i] = work.tile([P, E], F32, name="a")
-                    row_sums[i] = work.tile([P, 2], F32, name="row_sums")
-                nc.scalar.activation(
-                    out=a_tiles[i][:, half * BANK : (half + 1) * BANK],
-                    in_=bank[:],
-                    func=ACT.Sigmoid,
-                    accum_out=row_sums[i][:, half : half + 1],
-                )
-
-            def apply_gain(i, half):
-                if half == 0:
-                    h_tiles[i] = work.tile([P, E], BF16, name="h", align_bytes=64)
-                cols = slice(half * BANK, (half + 1) * BANK)
-                nc.vector.tensor_tensor(
-                    out=h_tiles[i][:, cols].rearrange("q (u p e) -> q u p e", u=2, e=2),
-                    in0=a_tiles[i][:, cols].rearrange("q (p u e) -> q u p e", u=2, e=2),
-                    in1=gain_all[:, cols].rearrange("q (u p e) -> q u p e", u=2, e=2),
-                    op=ALU.mult,
-                )
-
-            def finish_mean(i):
-                means[i] = work.tile([P, 1], F32, name="mean")
-                nc.vector.tensor_scalar(
-                    out=means[i][:], in0=row_sums[i][:, 0:1], scalar1=row_sums[i][:, 1:2], scalar2=1.0 / E, op0=ALU.add, op1=ALU.mult
-                )
-
-            def invert_mean(i):
-                nc.vector.reciprocal(out=inv_mean[i][:], in_=means[i][:])
-
-            h_grouped = {}
-
-            def transpose_h(i):
-                words = h_tiles[i][:].bitcast(F32)
-                bank = psum.tile([P, 2, 2, P], F32, name="bank")
-                for g in range(2):
-                    for u in range(2):
-                        first = P * (2 * g + u)
-                        nc.tensor.transpose(bank[:, g, u, :], words[:, first : first + P], ident[:])
-                h_grouped[i] = work.tile([P, E_PASSES, P, PACK], BF16, name="h_grouped", align_bytes=64)
-                dst = h_grouped[i][:].rearrange("p g r t -> p g (r t)").bitcast(F32)
-                nc.scalar.copy(out=dst.rearrange("p g (r u) -> p g r u", u=2), in_=bank[:].rearrange("p g u r -> p g r u"))
-
-            def quantise_h(i):
-                nc.vector.quantize_mx(
-                    out=h_codes[i][:].bitcast(E5M2X4),
-                    scales=h_planes[i][:],
-                    in_=h_grouped[i][:].rearrange("p g r t -> p (g r t)"),
-                )
-
-            def group_v(g, q):
-                v_grouped[g, q] = work.tile([P, BANK, PACK], BF16, name="v_grouped", align_bytes=64)
-                first = (q % 2) * BANK
-                nc.vector.tensor_copy(
-                    out=v_grouped[g, q][:],
-                    in_=v_raw[g][q // 2][:, :, first : first + BANK].rearrange("p j d -> p d j"),
-                )
-
-            def quantise_v(g, q):
-                nc.vector.quantize_mx(
-                    out=v_codes[g][q][:].bitcast(E4M3X4),
-                    scales=v_planes[g][q][:],
-                    in_=v_grouped[g, q][:].rearrange("p d j -> p (d j)"),
-                )
-
-            def mix(i, half, share, last=False):
-                y = work.tile([P, 2 * BANK], F32, name="y", bufs=8)
-                for qq in range(2):
-                    q = 2 * half + qq
-                    bank = psum.tile([P, BANK], F32, name="bank")
-                    for g in range(E_PASSES):
-                        rows = slice(g * P, (g + 1) * P)
-                        nc.tensor.matmul_mx(
-                            out=bank[:],
-                            lhsT=h_codes[i][:, rows].bitcast(E5M2X4),
-                            lhsT_scale=h_planes[i][:, rows],
-                            rhs=v_codes[g][q][:].bitcast(E4M3X4),
-                            rhs_scale=v_planes[g][q][:],
-                            start=(g == 0),
-                            stop=(g == E_PASSES - 1),
-                        )
-                    dst = y[:, qq * BANK : (qq + 1) * BANK]
-                    if qq == 0 or not share:
-                        nc.scalar.activation(out=dst, in_=bank[:], func=ACT.Copy, scale=inv_mean[i][:])
-                    else:
-                        nc.vector.tensor_scalar(out=dst, in0=bank[:], scalar1=inv_mean[i][:], scalar2=None, op0=ALU.mult)
-                    if last:
-                        nc.sync.dma_start(out=out[i * P : (i + 1) * P, q * BANK : (q + 1) * BANK], in_=dst)
-                if not last:
-                    nc.sync.dma_start(
-                        out=out[i * P : (i + 1) * P, half * 2 * BANK : (half + 1) * 2 * BANK], in_=y[:]
-                    )
-
+            dummy_matmuls(DUMMIES[0])
             transpose_x(0)
             quantise_x(0)
-            for g in range(2):
-                bank = psum.tile([P, BANK], F32, name="bank")
-                nc.tensor.matmul(bank[:], lhsT=ones[:], rhs=gain_row[:, g * BANK : (g + 1) * BANK], start=True, stop=True)
-                nc.vector.tensor_copy(
-                    out=gain_all[:, g * BANK : (g + 1) * BANK].rearrange("q (u p e) -> q u p e", u=2, e=2),
-                    in_=bank[:].rearrange("q (p u e) -> q u p e", u=2, e=2),
-                )
+            dummy_matmuls(DUMMIES[1])
             transpose_x(1)
+            dummy_matmuls(DUMMIES[2])
 
-            v_plan = {1: [(0, 0)], 2: [(0, 1), (1, 0)], 3: [(1, 1)], 4: [(0, 2)], 5: [(1, 2)], 6: [(0, 3)], 7: [(1, 3)]}
-            y_plan = {
-                4: [(0, 0)], 5: [(1, 0), (2, 0)], 6: [(3, 0), (4, 0)], 7: [(5, 0)],
-            }
+            pairs = [(i, 0) for i in range(6)] + [(i, 1) for i in range(3)]
+            pairs += [(i, 0) for i in range(6, TILES)] + [(i, 1) for i in range(3, TILES)]
+
             for s in range(TILES + 1):
-                units = v_plan.get(s, [])
+                pieces = [piece for piece in V_STEP if V_STEP[piece] == s]
+                tiles = slice(*MEANS_AFTER_STEP[s - 1]) if s - 1 in MEANS_AFTER_STEP else None
                 if s == 0:
                     for half in range(2):
-                        logits_passes(0, half, (0, 1))
-                    logits_passes(0, 0, (2, 3))
-                    affinities(0, 0)
+                        logits(0, half, (0, 1))
+                    logits(0, 0, (2, 3))
+                    sigmoid(0, 0)
                 elif s < TILES:
-                    logits_passes(s, 0, range(K_PASSES))
-                    affinities(s, 0)
-                if 1 <= s + 1 < TILES:
+                    logits(s, 0, range(X_PASSES))
+                    sigmoid(s, 0)
+                if s + 1 < TILES:
                     quantise_x(s + 1)
+                if tiles:
+                    divide_by_experts(tiles)
                 if s >= 2:
                     quantise_h(s - 2)
-                if units:
-                    group_v(*units[0])
+                for piece in pieces[:1]:
+                    interleave_v(*piece)
+                if tiles:
+                    invert_mean(tiles)
                 if s < TILES:
-                    logits_passes(s, 1, (2, 3) if s == 0 else range(K_PASSES))
-                    affinities(s, 1)
+                    logits(s, 1, (2, 3) if s == 0 else range(X_PASSES))
+                    sigmoid(s, 1)
+                    if s == 0:
+                        spread_gain()
                     apply_gain(s, 0)
-                if units:
-                    quantise_v(*units[0])
+                for piece in pieces[:1]:
+                    quantise_v(*piece)
                 if s + 2 < TILES:
                     transpose_x(s + 2)
-                if len(units) > 1:
-                    group_v(*units[1])
+                for piece in pieces[1:]:
+                    interleave_v(*piece)
                 if s < TILES:
                     apply_gain(s, 1)
-                    finish_mean(s)
+                if s in MEANS_AFTER_STEP:
+                    add_row_sums(slice(*MEANS_AFTER_STEP[s]))
                 if s >= 1:
                     transpose_h(s - 1)
-                if len(units) > 1:
-                    quantise_v(*units[1])
-                if s < TILES:
-                    invert_mean(s)
-                for i, half in y_plan.get(s, []):
-                    mix(i, half, False)
-            mix(6, 0, True)
-            mix(0, 1, True)
-            quantise_h(7)
-            mix(1, 1, True)
-            mix(7, 0, True)
-            for i in range(2, TILES):
-                mix(i, 1, True, i == TILES - 1)
+                for piece in pieces[1:]:
+                    quantise_v(*piece)
+                for n in range(MIXES_IN_STEP.get(s, 0)):
+                    mix(*pairs[0], ("scalar", "scalar"))
+                    pairs = pairs[1:]
+
+            for n, pair in enumerate(pairs):
+                if n == 1:
+                    quantise_h(TILES - 1)
+                mix(*pair, ("scalar", "vector"), store_quarters=(n == len(pairs) - 1))

from contextlib import ExitStack

import concourse.mybir as mybir
from concourse.masks import make_identity

M, K, E, D = 1024, 2048, 1024, 2048
FLOPS = 2 * M * K * E + 2 * M * E * D

F32 = mybir.dt.float32
BF16 = mybir.dt.bfloat16
I32 = mybir.dt.int32
U32 = mybir.dt.uint32
U8 = mybir.dt.uint8
E4M3X4 = mybir.dt.float8_e4m3fn_x4
E5M2X4 = mybir.dt.float8_e5m2_x4
E2M1X4 = mybir.dt.float4_e2m1fn_x4
SIGMOID = mybir.ActivationFunctionType.Sigmoid
COPY = mybir.ActivationFunctionType.Copy
ADD = mybir.AluOpType.add
MULT = mybir.AluOpType.mult

P = 128
PACK = 4
K_PASS = P * PACK
X_PASSES = K // K_PASS
H_PASSES = E // K_PASS
TILES = M // P
BANK = 512
QUARTERS = D // BANK
HALF = 2 * BANK

V_STEP = {(0, 0): 1, (1, 0): 2, (0, 1): 3, (1, 1): 3, (0, 2): 4, (1, 2): 5, (0, 3): 6, (1, 3): 7}
V_ON_SCALAR = (0, 2)
MIXES_IN_STEP = {4: 1, 5: 2, 6: 2, 7: 2}
MEANS_AFTER_STEP = {3: (0, 4), 5: (4, 6), 7: (6, 8)}
DUMMIES = (4, 1, 2)


def tile_sigmoid_router_bias_mix_s9_kernel(tc, x, w_words, w_scales, gain, v, out):
    nc = tc.nc
    with ExitStack() as ctx:
        keep = ctx.enter_context(tc.tile_pool(name="keep", bufs=1))
        work = ctx.enter_context(tc.tile_pool(name="work", bufs=3))
        psum = ctx.enter_context(tc.psum_pool(name="psum", bufs=8))

        x_raw = [keep.tile([P, K], BF16, name="x_raw_%d" % i, align_bytes=64) for i in range(TILES)]
        v_raw = [
            [keep.tile([P, PACK, HALF], BF16, name="v_raw_%d_%d" % (g, h), align_bytes=64) for h in range(D // HALF)]
            for g in range(H_PASSES)
        ]
        w_codes = keep.tile([P, X_PASSES, 2 * E], U8, name="w_codes", align_bytes=64)
        w_planes = keep.tile([P, X_PASSES, E], U8, name="w_planes", align_bytes=64)
        v_codes = [
            [keep.tile([P, BANK], U32, name="v_codes_%d_%d" % (g, q), align_bytes=64) for q in range(QUARTERS)]
            for g in range(H_PASSES)
        ]
        v_planes = [
            [keep.tile([P, BANK], U8, name="v_planes_%d_%d" % (g, q), align_bytes=64) for q in range(QUARTERS)]
            for g in range(H_PASSES)
        ]
        h_codes = [keep.tile([P, H_PASSES * P], U32, name="h_codes_%d" % i, align_bytes=64) for i in range(TILES)]
        h_planes = [keep.tile([P, H_PASSES * P], U8, name="h_planes_%d" % i, align_bytes=64) for i in range(TILES)]
        row_sums = keep.tile([P, H_PASSES, TILES], F32, name="row_sums")
        row_sum = keep.tile([P, TILES], F32, name="row_sum")
        mean = keep.tile([P, TILES], F32, name="mean")
        inv_mean = keep.tile([P, TILES], F32, name="inv_mean")
        gain_row = keep.tile([P, E], BF16, name="gain_row")
        gain_all = keep.tile([P, E], F32, name="gain_all")
        dummy_rhs = keep.tile([P, BANK], BF16, name="dummy_rhs")
        ones = keep.tile([P, P], BF16, name="ones")
        ident = keep.tile([P, P], F32, name="ident")
        table_loader = keep.tile([P, 1], F32, name="table_loader")

        x_grouped, x_codes, x_planes = {}, {}, {}
        logit_banks, affinity, h_tiles, h_grouped, v_grouped = {}, {}, {}, {}, {}


        def load_x(i, parts=1):
            width = K // parts
            for c in range(parts):
                cols = slice(c * width, (c + 1) * width)
                nc.sync.dma_start(out=x_raw[i][:, cols], in_=x[i * P : (i + 1) * P, cols])

        def load_w_scales():
            for quadrant in range(4):
                nc.sync.dma_start(
                    out=w_planes[32 * quadrant : 32 * quadrant + 4, :, :].bitcast(I32),
                    in_=w_scales[:, 4 * quadrant : 4 * quadrant + 4, :].rearrange("g r n -> r g n").bitcast(I32),
                )

        def load_w_pair(g):
            nc.sync.dma_start(
                out=w_codes[:, g : g + 2, :].bitcast(I32),
                in_=w_words[g : g + 2].rearrange("g p b -> p g b").bitcast(I32),
            )

        def load_v(g, h):
            piece = v[g * K_PASS : (g + 1) * K_PASS, h * HALF : (h + 1) * HALF]
            nc.sync.dma_start(out=v_raw[g][h][:], in_=piece.rearrange("(p j) d -> p j d", j=PACK))


        def dummy_matmuls(count):
            bank = psum.tile([P, BANK], F32, name="bank")
            for n in range(count):
                nc.tensor.matmul(bank[:], lhsT=ones[:], rhs=dummy_rhs[:], start=True, stop=True)

        def spread_gain():
            for g in range(H_PASSES):
                cols = slice(g * K_PASS, (g + 1) * K_PASS)
                bank = psum.tile([P, BANK], F32, name="bank")
                nc.tensor.matmul(bank[:], lhsT=ones[:], rhs=gain_row[:, cols], start=True, stop=True)
                nc.vector.tensor_copy(
                    out=gain_all[:, cols].rearrange("q (u p e) -> q u p e", u=2, e=2),
                    in_=bank[:].rearrange("q (p u e) -> q u p e", u=2, e=2),
                )


        def transpose_x(i):
            words = x_raw[i][:].bitcast(F32)
            x_grouped[i] = work.tile([P, X_PASSES, P, PACK], BF16, name="x_grouped", align_bytes=64)
            for pair in range(X_PASSES // 2):
                bank = psum.tile([P, 2, 2, P], F32, name="bank")
                for g in range(2):
                    for u in range(2):
                        first = (2 * pair + g) * K_PASS // 2 + u
                        nc.tensor.transpose(bank[:, g, u, :], words[:, first : first + K_PASS // 2 - 1 : 2], ident[:])
                grouped = x_grouped[i][:, 2 * pair : 2 * pair + 2].rearrange("p g r t -> p g (r t)").bitcast(F32)
                dst = grouped.rearrange("p g (r u) -> p g r u", u=2)
                src = bank[:].rearrange("p g u r -> p g r u")
                if i == 0 and pair == 0:
                    nc.vector.tensor_copy(out=dst, in_=src)
                else:
                    nc.scalar.copy(out=dst, in_=src)

        def quantise_x(i):
            x_codes[i] = work.tile([P, X_PASSES * P], U32, name="x_codes", align_bytes=64)
            x_planes[i] = work.tile([P, X_PASSES * P], U8, name="x_planes", align_bytes=64)
            nc.vector.quantize_mx(
                out=x_codes[i][:].bitcast(E4M3X4),
                scales=x_planes[i][:],
                in_=x_grouped[i][:].rearrange("p g r t -> p (g r t)"),
            )

        def logits(i, half, passes):
            if passes[0] == 0:
                logit_banks[half] = psum.tile([P, BANK], F32, name="bank")
            for g in passes:
                tokens = slice(g * P, (g + 1) * P)
                nc.tensor.matmul_mx(
                    out=logit_banks[half][:],
                    lhsT=x_codes[i][:, tokens].bitcast(E4M3X4),
                    lhsT_scale=x_planes[i][:, tokens],
                    rhs=w_codes[:, g, 2 * half * BANK : 2 * (half + 1) * BANK].bitcast(E2M1X4),
                    rhs_scale=w_planes[:, g, half * BANK : (half + 1) * BANK],
                    start=(g == 0),
                    stop=(g == X_PASSES - 1),
                )

        def sigmoid(i, half):
            if half == 0:
                affinity[i] = work.tile([P, E], F32, name="affinity")
            nc.scalar.activation(
                out=affinity[i][:, half * BANK : (half + 1) * BANK],
                in_=logit_banks[half][:],
                func=SIGMOID,
                accum_out=row_sums[:, half, i : i + 1],
            )

        def apply_gain(i, half):
            if half == 0:
                h_tiles[i] = work.tile([P, E], BF16, name="h", align_bytes=64)
            cols = slice(half * BANK, (half + 1) * BANK)
            nc.vector.tensor_tensor(
                out=h_tiles[i][:, cols].rearrange("q (u p e) -> q u p e", u=2, e=2),
                in0=affinity[i][:, cols].rearrange("q (p u e) -> q u p e", u=2, e=2),
                in1=gain_all[:, cols].rearrange("q (u p e) -> q u p e", u=2, e=2),
                op=MULT,
            )

        def add_row_sums(tiles):
            nc.vector.tensor_tensor(
                out=row_sum[:, tiles], in0=row_sums[:, 0, tiles], in1=row_sums[:, 1, tiles], op=ADD
            )

        def divide_by_experts(tiles):
            nc.vector.tensor_scalar(
                out=mean[:, tiles], in0=row_sum[:, tiles], scalar1=1.0 / E, scalar2=None, op0=MULT
            )

        def invert_mean(tiles):
            nc.vector.reciprocal(out=inv_mean[:, tiles], in_=mean[:, tiles])


        def transpose_h(i):
            words = h_tiles[i][:].bitcast(F32)
            bank = psum.tile([P, H_PASSES, 2, P], F32, name="bank")
            for g in range(H_PASSES):
                for u in range(2):
                    first = P * (2 * g + u)
                    nc.tensor.transpose(bank[:, g, u, :], words[:, first : first + P], ident[:])
            h_grouped[i] = work.tile([P, H_PASSES, P, PACK], BF16, name="h_grouped", align_bytes=64)
            grouped = h_grouped[i][:].rearrange("p g r t -> p g (r t)").bitcast(F32)
            nc.scalar.copy(out=grouped.rearrange("p g (r u) -> p g r u", u=2), in_=bank[:].rearrange("p g u r -> p g r u"))

        def quantise_h(i):
            nc.vector.quantize_mx(
                out=h_codes[i][:].bitcast(E5M2X4),
                scales=h_planes[i][:],
                in_=h_grouped[i][:].rearrange("p g r t -> p (g r t)"),
            )

        def interleave_v(g, q):
            v_grouped[g, q] = work.tile([P, BANK, PACK], BF16, name="v_grouped", align_bytes=64)
            first = (q % 2) * BANK
            copy = nc.scalar.copy if (g, q) == V_ON_SCALAR else nc.vector.tensor_copy
            copy(
                out=v_grouped[g, q][:].rearrange("p (c i) j -> p c j i", i=4),
                in_=v_raw[g][q // 2][:, :, first : first + BANK].rearrange("p j (c i) -> p c j i", i=4),
            )

        def quantise_v(g, q):
            nc.vector.quantize_mx(
                out=v_codes[g][q][:].bitcast(E4M3X4),
                scales=v_planes[g][q][:],
                in_=v_grouped[g, q][:].rearrange("p d j -> p (d j)"),
            )


        def mix(i, half, engines, store_quarters=False):
            rows = slice(i * P, (i + 1) * P)
            y = work.tile([P, HALF], F32, name="y", bufs=8)
            for b in range(2):
                q = 2 * half + b
                bank = psum.tile([P, BANK], F32, name="bank")
                for g in range(H_PASSES):
                    tokens = slice(g * P, (g + 1) * P)
                    nc.tensor.matmul_mx(
                        out=bank[:],
                        lhsT=h_codes[i][:, tokens].bitcast(E5M2X4),
                        lhsT_scale=h_planes[i][:, tokens],
                        rhs=v_codes[g][q][:].bitcast(E4M3X4),
                        rhs_scale=v_planes[g][q][:],
                        start=(g == 0),
                        stop=(g == H_PASSES - 1),
                    )
                dst = y[:, b * BANK : (b + 1) * BANK]
                inverse = inv_mean[:, i : i + 1]
                if engines[b] == "scalar":
                    nc.scalar.activation(out=dst, in_=bank[:], func=COPY, scale=inverse)
                else:
                    nc.vector.tensor_scalar(out=dst, in0=bank[:], scalar1=inverse, scalar2=None, op0=MULT)
                if store_quarters:
                    nc.sync.dma_start(out=out[rows, q * BANK : (q + 1) * BANK], in_=dst)
            if not store_quarters:
                nc.sync.dma_start(out=out[rows, half * HALF : (half + 1) * HALF], in_=y[:])


        with tc.manual_schedule():
            nc.vector.memset(table_loader[:], 0.0)
            make_identity(nc, ident[:])
            nc.vector.memset(ones[:], 1.0)
            nc.vector.memset(dummy_rhs[:], 0.0)
            nc.vector.memset(w_planes[:].rearrange("p g n -> p (g n)").bitcast(I32), 0)
            nc.vector.memset(gain_row[:], 0.0)
            nc.scalar.activation(out=table_loader[:], in_=table_loader[:], func=SIGMOID)

            load_x(0, parts=2)
            load_x(1)
            load_w_scales()
            load_w_pair(0)
            load_w_pair(2)
            nc.sync.dma_start(out=gain_row[0:1, :], in_=gain.rearrange("(o e) -> o e", o=1))
            load_x(2)
            load_x(3)
            load_v(0, 0)
            load_x(4)
            load_v(1, 0)
            for i in range(5, TILES):
                load_x(i)
            load_v(0, 1)
            load_v(1, 1)

            dummy_matmuls(DUMMIES[0])
            transpose_x(0)
            quantise_x(0)
            dummy_matmuls(DUMMIES[1])
            transpose_x(1)
            dummy_matmuls(DUMMIES[2])

            pairs = [(i, 0) for i in range(6)] + [(i, 1) for i in range(3)]
            pairs += [(i, 0) for i in range(6, TILES)] + [(i, 1) for i in range(3, TILES)]

            for s in range(TILES + 1):
                pieces = [piece for piece in V_STEP if V_STEP[piece] == s]
                tiles = slice(*MEANS_AFTER_STEP[s - 1]) if s - 1 in MEANS_AFTER_STEP else None
                if s == 0:
                    for half in range(2):
                        logits(0, half, (0, 1))
                    logits(0, 0, (2, 3))
                    sigmoid(0, 0)
                elif s < TILES:
                    logits(s, 0, range(X_PASSES))
                    sigmoid(s, 0)
                if s + 1 < TILES:
                    quantise_x(s + 1)
                if tiles:
                    divide_by_experts(tiles)
                if s >= 2:
                    quantise_h(s - 2)
                for piece in pieces[:1]:
                    interleave_v(*piece)
                if tiles:
                    invert_mean(tiles)
                if s < TILES:
                    logits(s, 1, (2, 3) if s == 0 else range(X_PASSES))
                    sigmoid(s, 1)
                    if s == 0:
                        spread_gain()
                    apply_gain(s, 0)
                for piece in pieces[:1]:
                    quantise_v(*piece)
                if s + 2 < TILES:
                    transpose_x(s + 2)
                for piece in pieces[1:]:
                    interleave_v(*piece)
                if s < TILES:
                    apply_gain(s, 1)
                if s in MEANS_AFTER_STEP:
                    add_row_sums(slice(*MEANS_AFTER_STEP[s]))
                if s >= 1:
                    transpose_h(s - 1)
                for piece in pieces[1:]:
                    quantise_v(*piece)
                for n in range(MIXES_IN_STEP.get(s, 0)):
                    mix(*pairs[0], ("scalar", "scalar"))
                    pairs = pairs[1:]

            for n, pair in enumerate(pairs):
                if n == 1:
                    quantise_h(TILES - 1)
                mix(*pair, ("scalar", "vector"), store_quarters=(n == len(pairs) - 1))
